import numpy as np
CORES = [0,1,2,3,4,5,6,7,8,9,10,11,12,13,14,15,16,17,18,19,20,21,22,23,24,25,26,27,28,29,30,31,32,33,34,35,36,37,38,39,40,41,42,43,44,45,46,47,48,49,50,51,52,53,54,55,56,57,58,59,60,61,62,63,64,65,66,67,68,69,70,71,72,73,74,75,76,77,78,79,80,81,82,83,84,85,86,87,88,89,90,91,92,93,94,95,96,97,98,99,100,101,102,103,104,105,106,107,108,109,110,111,112,113,114,115,116,117,118,119,120,121,122,123,124,125,126,127,128,129,130,131,132,133,134,135,136,137,138,139,140,141,142,143,144,145,146,147,148,149,150,151,152,153,154,155,156,157,158,159,160,161,162,163,164,165,166,167,168,169,170,171,172,173,174,175,176,177,178,179,180,181,182,183,184,185,186,187,188,189,190,191,192,193,194,195,196,197,198,199,200,201,202,203,204,205,206,207,208,209,210,211,212,213,214,215,216,217,218,219,220,221,222,223,224,225,226,227,228,229,230,231,232,233,234,235,236,237,238,239,240,241,242,243,244,245,246,247,248,249,250,251,252,253,254,255]
N = 256
def setup_inputs(rng):
    return {"x": rng.standard_normal((N, 128, 1024), dtype=np.float32).astype(np.float32)}
def reference(x):
    s = x.sum(axis=0, dtype=np.float64).astype(x.dtype)
    return {"y": np.broadcast_to(s, (N,) + s.shape)}

@@ -1,0 +1,110 @@
+from concourse.bass import DstId, RemoteDMATransfer
+
+P = (0, 1, 4, 5)
+M = (2, 3, 6, 7)
+B = 128
+W = 16
+
+SCRATCH = {
+    "xs": ("sbuf", [128, 1024], "float32"),
+    "out": ("sbuf", [128, 1024], "float32"),
+    "l1": ("sbuf", [128, 7 * B], "float32"),
+    "ml": ("sbuf", [128, B], "float32"),
+    "hl": ("sbuf", [128, 7 * W], "float32"),
+    "ex": ("sbuf", [128, W], "float32"),
+}
+SEMAPHORES = ["loaded", "sent", "a", "b", "c", "d", "e", "f", "z", "stored"]
+
+
+def rank_program(g, core, T, topo):
+    h, ch, k = topo.host(core), topo.chip(core), core % 8
+    par, q = ch & 1, ch >> 1
+    own, oth = 512 * par, 512 * (1 - par)
+    S = T.sem
+
+    def world(hh, cc, kk):
+        return hh * 128 + cc * 8 + kk
+
+    def did(dst):
+        rid, pid = topo.addr(dst, core)
+        return DstId(rid=rid, pnc=pid)
+
+    def blk(j):
+        return own + B * P.index(j) if j in P else oth + B * M.index(j)
+
+    sent = 0
+    is_p = k in P
+    b = P.index(k) if is_p else M.index(k)
+    others = [j for j in range(8) if j != k]
+
+    g.dma_start(out=T.xs[:], in_=T.x[:]).then_inc(S.loaded, 16)
+    g.wait_ge(S.loaded, 16)
+
+    tr = []
+    for i, j in enumerate(others):
+        slot = k if k < j else k - 1
+        tr.append(RemoteDMATransfer(dst_ids=[did(world(h, ch, j))], dma_engine_mask=3 << (2 * i), remote_sem=S.a,
+                                    src=T.xs[:, blk(j):blk(j) + B], dst=T.l1[:, slot * B:(slot + 1) * B]))
+    g.remote_dma_fused(tr, local_sem=S.sent)
+    sent += 14
+    g.wait_ge(S.a, 14)
+
+    def copies(lo, n):
+        c0 = blk(k) + lo
+        return [T.xs[:, c0:c0 + n]] + [T.l1[:, s * B + lo:s * B + lo + n] for s in range(7)]
+
+    if not is_p:
+        g.remote_dma_fused([RemoteDMATransfer(dst_ids=[did(world(h, ch ^ 1, P[b]))], dma_engine_mask=0xFF,
+                                              remote_sem=S.b, srcs=copies(0, B), dsts=[T.ml[:]], alu_op=1)],
+                           local_sem=S.sent)
+        sent += 8
+        g.wait_ge(S.e, 64)
+        c0 = own + B * b
+        fin = T.out[:, c0:c0 + B]
+        g.remote_dma_fused([
+            RemoteDMATransfer(dst_ids=[did(world(h, ch ^ 1, P[b]))], dma_engine_mask=0x00FF, remote_sem=S.f,
+                              src=fin, dst=fin),
+            RemoteDMATransfer(dst_ids=[did(world(h, ch, j)) for j in others], dma_engine_mask=0xFF00, remote_sem=S.z,
+                              srcs=[fin], dsts=[fin for j in others]),
+        ], local_sem=S.sent)
+        sent += 16
+        g.wait_ge(S.z, 4 * 16 + 3 * 8)
+    else:
+        g.wait_ge(S.b, 8)
+
+        def copies9(lo, n):
+            return copies(lo, n) + [T.ml[:, lo:lo + n]]
+
+        tr = []
+        for i, qq in enumerate([x for x in range(8) if x != q]):
+            slot = q if q < qq else q - 1
+            tr.append(RemoteDMATransfer(dst_ids=[did(world(h, 2 * qq + par, k))], dma_engine_mask=1 << i,
+                                        remote_sem=S.c, srcs=copies9(qq * W, W),
+                                        dsts=[T.hl[:, slot * W:(slot + 1) * W]], alu_op=1))
+        g.remote_dma_fused(tr, local_sem=S.sent)
+        sent += 7
+        g.wait_ge(S.c, 7)
+        mine = copies9(q * W, W) + [T.hl[:, s * W:(s + 1) * W] for s in range(7)]
+        g.remote_dma_fused([RemoteDMATransfer(dst_ids=[did(world(1 - h, ch, k))], dma_engine_mask=0xFF,
+                                              remote_sem=S.d, srcs=mine, dsts=[T.ex[:]], alu_op=1)],
+                           local_sem=S.sent)
+        sent += 8
+        g.wait_ge(S.d, 8)
+        c0 = own + B * b + W * q
+        g.remote_dma_fused([RemoteDMATransfer(dst_ids=[did(world(h, 2 * qq + par, M[b])) for qq in range(8)],
+                                              dma_engine_mask=0xFF, remote_sem=S.e, srcs=mine + [T.ex[:]],
+                                              dsts=[T.out[:, c0:c0 + W] for qq in range(8)], alu_op=1)],
+                           local_sem=S.sent)
+        sent += 8
+        g.wait_ge(S.f, 8)
+        c0 = oth + B * b
+        fin = T.out[:, c0:c0 + B]
+        g.remote_dma_fused([RemoteDMATransfer(dst_ids=[did(world(h, ch, j)) for j in others], dma_engine_mask=0xFFFF,
+                                              remote_sem=S.z, srcs=[fin], dsts=[fin for j in others])],
+                           local_sem=S.sent)
+        sent += 16
+        g.wait_ge(S.z, 3 * 16 + 4 * 8)
+
+    g.dma_start(out=T.y[:], in_=T.out[:]).then_inc(S.stored, 16)
+    g.wait_ge(S.stored, 16)
+    g.wait_ge(S.sent, sent)

@@ -2,24 +2,22 @@ from concourse.bass import DstId, RemoteDMATransfer
 
 P = (0, 1, 4, 5)
 M = (2, 3, 6, 7)
-B = 128
-W = 16
+R = 128
 
 SCRATCH = {
-    "xs": ("sbuf", [128, 1024], "float32"),
-    "out": ("sbuf", [128, 1024], "float32"),
-    "l1": ("sbuf", [128, 7 * B], "float32"),
-    "ml": ("sbuf", [128, B], "float32"),
-    "hl": ("sbuf", [128, 7 * W], "float32"),
-    "ex": ("sbuf", [128, W], "float32"),
+    "xl": ("dram", [16 * R, 128], "float32"),
+    "lf": ("dram", [96 * R, 16], "float32"),
+    "hs": ("dram", [2 * R, 16], "float32"),
+    "out": ("dram", [8 * R, 128], "float32"),
 }
-SEMAPHORES = ["loaded", "sent", "a", "b", "c", "d", "e", "f", "z", "stored"]
+SEMAPHORES = ["loaded", "sent", "a", "b", "c", "d", "e", "f", "z", "moved", "stored"]
 
 
 def rank_program(g, core, T, topo):
     h, ch, k = topo.host(core), topo.chip(core), core % 8
     par, q = ch & 1, ch >> 1
-    own, oth = 512 * par, 512 * (1 - par)
+    own, oth = 4 * par, 4 * (1 - par)
+    xb, sb = (0, 8) if par else (8, 0)
     S = T.sem
 
     def world(hh, cc, kk):
@@ -30,37 +28,75 @@ def rank_program(g, core, T, topo):
         return DstId(rid=rid, pnc=pid)
 
     def blk(j):
-        return own + B * P.index(j) if j in P else oth + B * M.index(j)
+        return own + P.index(j) if j in P else oth + M.index(j)
+
+    def rows(t, i):
+        return t[i * R:(i + 1) * R, :]
 
     sent = 0
     is_p = k in P
     b = P.index(k) if is_p else M.index(k)
     others = [j for j in range(8) if j != k]
+    mine = xb + blk(k)
 
-    g.dma_start(out=T.xs[:], in_=T.x[:]).then_inc(S.loaded, 16)
+    g.dma_start(out=T.xl[xb * R:(xb + 8) * R, :], in_=T.x[:]).then_inc(S.loaded, 16)
     g.wait_ge(S.loaded, 16)
 
     tr = []
     for i, j in enumerate(others):
         slot = k if k < j else k - 1
         tr.append(RemoteDMATransfer(dst_ids=[did(world(h, ch, j))], dma_engine_mask=3 << (2 * i), remote_sem=S.a,
-                                    src=T.xs[:, blk(j):blk(j) + B], dst=T.l1[:, slot * B:(slot + 1) * B]))
+                                    src=rows(T.xl, xb + blk(j)), dst=rows(T.xl, sb + slot)))
     g.remote_dma_fused(tr, local_sem=S.sent)
     sent += 14
     g.wait_ge(S.a, 14)
 
-    def copies(lo, n):
-        c0 = blk(k) + lo
-        return [T.xs[:, c0:c0 + n]] + [T.l1[:, s * B + lo:s * B + lo + n] for s in range(7)]
-
-    if not is_p:
+    if is_p:
+        g.wait_ge(S.b, 8)
+        lo, hi = (mine, 16) if par else (0, mine + 1)
+        g.dma_start(out=T.lf[0:(hi - lo) * 8 * R, :], in_=T.xl[lo * R:hi * R, :]).then_inc(S.moved, 16)
+        g.wait_ge(S.moved, 16)
+        copies = [mine - lo] + [sb + s - lo for s in range(8)]
+        tr = []
+        for qq in range(8):
+            eng = 8 if qq == q else (qq if qq < q else qq - 1)
+            tr.append(RemoteDMATransfer(dst_ids=[did(world(h, 2 * qq + par, M[b]))], dma_engine_mask=1 << eng,
+                                        remote_sem=S.c, srcs=[rows(T.lf, 8 * t + qq) for t in copies],
+                                        dsts=[rows(T.lf, q)], alu_op=1))
+        g.remote_dma_fused(tr, local_sem=S.sent)
+        sent += 8
+        g.wait_ge(S.d, 16)
+        g.remote_dma_fused([RemoteDMATransfer(dst_ids=[did(world(h, 2 * qq + par, M[b])) for qq in range(8)],
+                                              dma_engine_mask=0xFF, remote_sem=S.e,
+                                              srcs=[rows(T.hs, 0), rows(T.hs, 1)],
+                                              dsts=[rows(T.lf, 8 + q) for qq in range(8)], alu_op=1)],
+                           local_sem=S.sent)
+        sent += 8
+        g.wait_ge(S.f, 8)
+        fin = rows(T.out, oth + b)
+        g.remote_dma_fused([RemoteDMATransfer(dst_ids=[did(world(h, ch, j)) for j in others], dma_engine_mask=0xFFFF,
+                                              remote_sem=S.z, srcs=[fin], dsts=[fin for j in others])],
+                           local_sem=S.sent)
+        sent += 16
+        g.wait_ge(S.z, 3 * 16 + 4 * 8)
+    else:
         g.remote_dma_fused([RemoteDMATransfer(dst_ids=[did(world(h, ch ^ 1, P[b]))], dma_engine_mask=0xFF,
-                                              remote_sem=S.b, srcs=copies(0, B), dsts=[T.ml[:]], alu_op=1)],
+                                              remote_sem=S.b,
+                                              srcs=[rows(T.xl, mine)] + [rows(T.xl, sb + s) for s in range(7)],
+                                              dsts=[rows(T.xl, xb + 7)], alu_op=1)],
+                           local_sem=S.sent)
+        sent += 8
+        g.wait_ge(S.c, 8)
+        g.remote_dma_fused([RemoteDMATransfer(dst_ids=[did(world(h, ch, P[b])), did(world(1 - h, ch, P[b]))],
+                                              dma_engine_mask=0xFF, remote_sem=S.d,
+                                              srcs=[rows(T.lf, s) for s in range(8)],
+                                              dsts=[rows(T.hs, 0), rows(T.hs, 1)], alu_op=1)],
                            local_sem=S.sent)
         sent += 8
         g.wait_ge(S.e, 64)
-        c0 = own + B * b
-        fin = T.out[:, c0:c0 + B]
+        fin = rows(T.out, own + b)
+        g.dma_start(out=fin, in_=T.lf[8 * R:16 * R, :]).then_inc(S.moved, 16)
+        g.wait_ge(S.moved, 16)
         g.remote_dma_fused([
             RemoteDMATransfer(dst_ids=[did(world(h, ch ^ 1, P[b]))], dma_engine_mask=0x00FF, remote_sem=S.f,
                               src=fin, dst=fin),
@@ -69,41 +105,6 @@ def rank_program(g, core, T, topo):
         ], local_sem=S.sent)
         sent += 16
         g.wait_ge(S.z, 4 * 16 + 3 * 8)
-    else:
-        g.wait_ge(S.b, 8)
-
-        def copies9(lo, n):
-            return copies(lo, n) + [T.ml[:, lo:lo + n]]
-
-        tr = []
-        for i, qq in enumerate([x for x in range(8) if x != q]):
-            slot = q if q < qq else q - 1
-            tr.append(RemoteDMATransfer(dst_ids=[did(world(h, 2 * qq + par, k))], dma_engine_mask=1 << i,
-                                        remote_sem=S.c, srcs=copies9(qq * W, W),
-                                        dsts=[T.hl[:, slot * W:(slot + 1) * W]], alu_op=1))
-        g.remote_dma_fused(tr, local_sem=S.sent)
-        sent += 7
-        g.wait_ge(S.c, 7)
-        mine = copies9(q * W, W) + [T.hl[:, s * W:(s + 1) * W] for s in range(7)]
-        g.remote_dma_fused([RemoteDMATransfer(dst_ids=[did(world(1 - h, ch, k))], dma_engine_mask=0xFF,
-                                              remote_sem=S.d, srcs=mine, dsts=[T.ex[:]], alu_op=1)],
-                           local_sem=S.sent)
-        sent += 8
-        g.wait_ge(S.d, 8)
-        c0 = own + B * b + W * q
-        g.remote_dma_fused([RemoteDMATransfer(dst_ids=[did(world(h, 2 * qq + par, M[b])) for qq in range(8)],
-                                              dma_engine_mask=0xFF, remote_sem=S.e, srcs=mine + [T.ex[:]],
-                                              dsts=[T.out[:, c0:c0 + W] for qq in range(8)], alu_op=1)],
-                           local_sem=S.sent)
-        sent += 8
-        g.wait_ge(S.f, 8)
-        c0 = oth + B * b
-        fin = T.out[:, c0:c0 + B]
-        g.remote_dma_fused([RemoteDMATransfer(dst_ids=[did(world(h, ch, j)) for j in others], dma_engine_mask=0xFFFF,
-                                              remote_sem=S.z, srcs=[fin], dsts=[fin for j in others])],
-                           local_sem=S.sent)
-        sent += 16
-        g.wait_ge(S.z, 3 * 16 + 4 * 8)
 
     g.dma_start(out=T.y[:], in_=T.out[:]).then_inc(S.stored, 16)
     g.wait_ge(S.stored, 16)

from concourse.bass import DstId, RemoteDMATransfer

P = (0, 1, 4, 5)
M = (2, 3, 6, 7)
R = 128

SCRATCH = {
    "xl": ("dram", [16 * R, 128], "float32"),
    "lf": ("dram", [96 * R, 16], "float32"),
    "hs": ("dram", [2 * R, 16], "float32"),
    "out": ("dram", [8 * R, 128], "float32"),
}
SEMAPHORES = ["loaded", "sent", "a", "b", "c", "d", "e", "f", "z", "moved", "stored"]


def rank_program(g, core, T, topo):
    h, ch, k = topo.host(core), topo.chip(core), core % 8
    par, q = ch & 1, ch >> 1
    own, oth = 4 * par, 4 * (1 - par)
    xb, sb = (0, 8) if par else (8, 0)
    S = T.sem

    def world(hh, cc, kk):
        return hh * 128 + cc * 8 + kk

    def did(dst):
        rid, pid = topo.addr(dst, core)
        return DstId(rid=rid, pnc=pid)

    def blk(j):
        return own + P.index(j) if j in P else oth + M.index(j)

    def rows(t, i):
        return t[i * R:(i + 1) * R, :]

    sent = 0
    is_p = k in P
    b = P.index(k) if is_p else M.index(k)
    others = [j for j in range(8) if j != k]
    mine = xb + blk(k)

    g.dma_start(out=T.xl[xb * R:(xb + 8) * R, :], in_=T.x[:]).then_inc(S.loaded, 16)
    g.wait_ge(S.loaded, 16)

    tr = []
    for i, j in enumerate(others):
        slot = k if k < j else k - 1
        tr.append(RemoteDMATransfer(dst_ids=[did(world(h, ch, j))], dma_engine_mask=3 << (2 * i), remote_sem=S.a,
                                    src=rows(T.xl, xb + blk(j)), dst=rows(T.xl, sb + slot)))
    g.remote_dma_fused(tr, local_sem=S.sent)
    sent += 14
    g.wait_ge(S.a, 14)

    if is_p:
        g.wait_ge(S.b, 8)
        lo, hi = (mine, 16) if par else (0, mine + 1)
        g.dma_start(out=T.lf[0:(hi - lo) * 8 * R, :], in_=T.xl[lo * R:hi * R, :]).then_inc(S.moved, 16)
        g.wait_ge(S.moved, 16)
        copies = [mine - lo] + [sb + s - lo for s in range(8)]
        tr = []
        for qq in range(8):
            eng = 8 if qq == q else (qq if qq < q else qq - 1)
            tr.append(RemoteDMATransfer(dst_ids=[did(world(h, 2 * qq + par, M[b]))], dma_engine_mask=1 << eng,
                                        remote_sem=S.c, srcs=[rows(T.lf, 8 * t + qq) for t in copies],
                                        dsts=[rows(T.lf, q)], alu_op=1))
        g.remote_dma_fused(tr, local_sem=S.sent)
        sent += 8
        g.wait_ge(S.d, 16)
        g.remote_dma_fused([RemoteDMATransfer(dst_ids=[did(world(h, 2 * qq + par, M[b])) for qq in range(8)],
                                              dma_engine_mask=0xFF, remote_sem=S.e,
                                              srcs=[rows(T.hs, 0), rows(T.hs, 1)],
                                              dsts=[rows(T.lf, 8 + q) for qq in range(8)], alu_op=1)],
                           local_sem=S.sent)
        sent += 8
        g.wait_ge(S.f, 8)
        fin = rows(T.out, oth + b)
        g.remote_dma_fused([RemoteDMATransfer(dst_ids=[did(world(h, ch, j)) for j in others], dma_engine_mask=0xFFFF,
                                              remote_sem=S.z, srcs=[fin], dsts=[fin for j in others])],
                           local_sem=S.sent)
        sent += 16
        g.wait_ge(S.z, 3 * 16 + 4 * 8)
    else:
        g.remote_dma_fused([RemoteDMATransfer(dst_ids=[did(world(h, ch ^ 1, P[b]))], dma_engine_mask=0xFF,
                                              remote_sem=S.b,
                                              srcs=[rows(T.xl, mine)] + [rows(T.xl, sb + s) for s in range(7)],
                                              dsts=[rows(T.xl, xb + 7)], alu_op=1)],
                           local_sem=S.sent)
        sent += 8
        g.wait_ge(S.c, 8)
        g.remote_dma_fused([RemoteDMATransfer(dst_ids=[did(world(h, ch, P[b])), did(world(1 - h, ch, P[b]))],
                                              dma_engine_mask=0xFF, remote_sem=S.d,
                                              srcs=[rows(T.lf, s) for s in range(8)],
                                              dsts=[rows(T.hs, 0), rows(T.hs, 1)], alu_op=1)],
                           local_sem=S.sent)
        sent += 8
        g.wait_ge(S.e, 64)
        fin = rows(T.out, own + b)
        g.dma_start(out=fin, in_=T.lf[8 * R:16 * R, :]).then_inc(S.moved, 16)
        g.wait_ge(S.moved, 16)
        g.remote_dma_fused([
            RemoteDMATransfer(dst_ids=[did(world(h, ch ^ 1, P[b]))], dma_engine_mask=0x00FF, remote_sem=S.f,
                              src=fin, dst=fin),
            RemoteDMATransfer(dst_ids=[did(world(h, ch, j)) for j in others], dma_engine_mask=0xFF00, remote_sem=S.z,
                              srcs=[fin], dsts=[fin for j in others]),
        ], local_sem=S.sent)
        sent += 16
        g.wait_ge(S.z, 4 * 16 + 3 * 8)

    g.dma_start(out=T.y[:], in_=T.out[:]).then_inc(S.stored, 16)
    g.wait_ge(S.stored, 16)
    g.wait_ge(S.sent, sent)
